import numpy as np, ml_dtypes
CORES = [45,53,77,117,47,55,79,119]
N = 8
DEG, TK = 3, 512
MASK = [[7,0,1],[0,1,2],[1,2,3],[2,3,4],[3,4,5],[4,5,6],[5,6,7],[6,7,0]]
def setup_inputs(rng):
    return {"x": rng.standard_normal((N, 128, TK), dtype=np.float32).astype(ml_dtypes.bfloat16), "w": rng.standard_normal((N, 128, DEG * 128), dtype=np.float32).astype(ml_dtypes.bfloat16)}
def setup_inputs_big(rng):
    d = setup_inputs(rng)
    for k in ("x", "w"): d[k] = (d[k].astype(np.float32) * 1024.0).astype(d[k].dtype)
    return d
def setup_inputs_small(rng):
    d = setup_inputs(rng)
    for k in ("x", "w"): d[k] = (d[k].astype(np.float32) * (1 / 1024.0)).astype(d[k].dtype)
    return d
def setup_inputs_apart(rng):
    d = setup_inputs(rng)
    f = (10.0 ** rng.permutation(np.linspace(-1.5, 1.5, N))).astype(np.float32).reshape(N, 1, 1)
    for k in ("x", "w"): d[k] = (d[k].astype(np.float32) * f).astype(d[k].dtype)
    return d
def reference(x, w):
    X, W = x.astype(np.float64), w.astype(np.float64)
    y = np.zeros((N, 128, TK))
    for r in range(N):
        for i, j in enumerate(MASK[r]):
            y[r] += W[r][:, 128 * i:128 * i + 128].T @ X[j]
    return {"y": y.astype(ml_dtypes.bfloat16 if x.dtype != np.float64 else np.float64)}

@@ -1,0 +1,123 @@
+from concourse.bass import DstId, RemoteDMATransfer
+
+TK = 512
+PIECES = 1
+VIA = ["helper"]
+E_DIRECT = 4
+E_HOP1 = 4
+E_HELPER = 8
+E_RANK = 4
+W = TK // PIECES
+
+SCRATCH = {
+    "xin0": ("sbuf", [128, TK], "bfloat16"),
+    "xin1": ("sbuf", [128, TK], "bfloat16"),
+    "xin2": ("sbuf", [128, TK], "bfloat16"),
+    "ws": ("sbuf", [128, 384], "bfloat16"),
+    "ys": ("sbuf", [128, TK], "bfloat16"),
+    "ps": ("psum", [128, TK], "float32"),
+    "xd": ("dram", [128, TK], "bfloat16"),
+    "hd": ("dram", [128, W], "bfloat16"),
+}
+SEMAPHORES = ["staged", "xl", "wl", "a0", "a1", "a2", "ha", "sent", "mm", "cp", "st"]
+
+
+def _engines(mask, first, n):
+    bits = [b for b in range(mask.bit_length()) if (mask >> b) & 1]
+    return sum(1 << b for b in bits[first:first + n])
+
+
+def _plan(T, topo):
+    cores = list(T.cores)
+    M = T.tables["MASK"]
+    flows = []
+    for j, c in enumerate(cores):
+        dests = sorted((row.index(j), r) for r, row in enumerate(M) if r != j and j in row)
+        if all(topo.may_write(c, cores[r]) for _, r in dests):
+            flows += [dict(j=j, r=r, slot=s, lo=0, hi=TK, via=None, n=E_DIRECT) for s, r in dests]
+            continue
+        local = [h for h in range(topo.CHIPS * topo.CORES_PER_CHIP) if topo.chip(h) == topo.chip(c) and h != c]
+        taken = []
+        for p in range(PIECES):
+            for s, r in dests:
+                ok = [h for h in local if topo.may_write(h, cores[r])]
+                if VIA[p] == "rank":
+                    pick, n = [h for h in ok if h in cores][0], E_RANK
+                else:
+                    dies = [topo.die(q) for q in taken]
+                    free = [h for h in ok if h not in cores and h not in taken]
+                    free.sort(key=lambda h: (topo.die(h) in dies, topo.die(h) != topo.die(c), h))
+                    pick, n = free[0], E_HELPER
+                    taken.append(pick)
+                flows.append(dict(j=j, r=r, slot=s, lo=p * W, hi=p * W + W, via=pick, n=n))
+    return flows
+
+
+def _send(g, core, T, topo, items):
+    trs, first = [], 0
+    for dst, out, src, sem, n in items:
+        rid, pid, _ = topo.addr(dst)
+        trs.append(RemoteDMATransfer(dst_ids=[DstId(rid=rid, pnc=pid)], dma_engine_mask=_engines(topo.mask(core, dst), first, n),
+                                     remote_sem=sem, src=src, dst=out))
+        first += n
+    g.remote_dma_fused(trs, local_sem=T.sem.sent)
+    return first
+
+
+def rank_program(g, core, T, topo):
+    flows = _plan(T, topo)
+    cores = list(T.cores)
+    S = T.sem
+    rank = T.rank_of(core)
+    relay = [f for f in flows if f["via"] == core]
+    if rank is None and not relay:
+        return
+    sent = 0
+
+    if rank is not None:
+        row = T.tables["MASK"][rank]
+        own = row.index(rank)
+        xs = T["xin%d" % own]
+        if PIECES == 1:
+            g.sync.dma_start(T.xd[:], T.x[:]).then_inc(S.staged, 16)
+        g.sync.dma_start(xs[:], T.x[:]).then_inc(S.xl, 16)
+        g.sync.dma_start(T.ws[:], T.w[:]).then_inc(S.wl, 16)
+
+        if PIECES == 1:
+            g.wait_ge(S.staged, 16)
+        else:
+            g.wait_ge(S.xl, 16)
+        mine = [f for f in flows if f["j"] == rank]
+        items, seen = [], []
+        for f in mine:
+            src = T.xd[:] if PIECES == 1 else xs[:, f["lo"]:f["hi"]]
+            if f["via"] is None:
+                items.append((cores[f["r"]], T["xin%d" % f["slot"]][:], src, S["a%d" % f["slot"]], f["n"]))
+            elif (f["via"], f["lo"]) not in seen:
+                seen.append((f["via"], f["lo"]))
+                items.append((f["via"], T.hd[:], src, S.ha, E_HOP1))
+        sent += _send(g, core, T, topo, items)
+
+    if relay:
+        g.wait_ge(S.ha, E_HOP1)
+        sent += _send(g, core, T, topo, [(cores[f["r"]], T["xin%d" % f["slot"]][:, f["lo"]:f["hi"]], T.hd[:],
+                                          S["a%d" % f["slot"]], f["n"]) for f in relay])
+    g.wait_ge(S.sent, sent)
+    if rank is None:
+        return
+
+    inc = [f for f in flows if f["r"] == rank]
+    late = {s: max(f["via"] is not None for f in inc if f["slot"] == s) for s in range(len(row)) if s != own}
+    order = [own] + sorted(late, key=lambda s: (late[s], s))
+    g.tensor.wait_ge(S.xl, 16)
+    g.tensor.wait_ge(S.wl, 16)
+    for k, s in enumerate(order):
+        if s != own:
+            g.tensor.wait_ge(S["a%d" % s], sum(f["n"] for f in inc if f["slot"] == s))
+        mm = g.tensor.matmul(T.ps[:], T.ws[:, 128 * s:128 * s + 128], T["xin%d" % s][:], k == 0, k == len(order) - 1)
+    mm.then_inc(S.mm, 1)
+    g.vector.wait_ge(S.mm, 1)
+    g.vector.tensor_copy(T.ys[:], T.ps[:]).then_inc(S.cp, 1)
+    g.sync.wait_ge(S.cp, 1)
+    g.sync.dma_start(T.y[:], T.ys[:]).then_inc(S.st, 16)
+    g.sync.wait_ge(S.st, 16)

@@ -1,13 +1,11 @@
 from concourse.bass import DstId, RemoteDMATransfer
 
 TK = 512
-PIECES = 1
-VIA = ["helper"]
+NP = 2
+W = TK // NP
 E_DIRECT = 4
-E_HOP1 = 4
+E_HOP1 = 8
 E_HELPER = 8
-E_RANK = 4
-W = TK // PIECES
 
 SCRATCH = {
     "xin0": ("sbuf", [128, TK], "bfloat16"),
@@ -15,11 +13,12 @@ SCRATCH = {
     "xin2": ("sbuf", [128, TK], "bfloat16"),
     "ws": ("sbuf", [128, 384], "bfloat16"),
     "ys": ("sbuf", [128, TK], "bfloat16"),
-    "ps": ("psum", [128, TK], "float32"),
-    "xd": ("dram", [128, TK], "bfloat16"),
-    "hd": ("dram", [128, W], "bfloat16"),
+    "hs": ("sbuf", [128, TK], "bfloat16"),
 }
-SEMAPHORES = ["staged", "xl", "wl", "a0", "a1", "a2", "ha", "sent", "mm", "cp", "st"]
+SEMAPHORES = ["wl", "sent"]
+for _p in range(NP):
+    SCRATCH["ps%d" % _p] = ("psum", [128, 512], "float32")
+    SEMAPHORES += [n % _p for n in ("xl%d", "ha%d", "a0p%d", "a1p%d", "a2p%d", "mm%d", "cp%d", "st%d")]
 
 
 def _engines(mask, first, n):
@@ -29,27 +28,20 @@ def _engines(mask, first, n):
 
 def _plan(T, topo):
     cores = list(T.cores)
-    M = T.tables["MASK"]
     flows = []
     for j, c in enumerate(cores):
-        dests = sorted((row.index(j), r) for r, row in enumerate(M) if r != j and j in row)
-        if all(topo.may_write(c, cores[r]) for _, r in dests):
-            flows += [dict(j=j, r=r, slot=s, lo=0, hi=TK, via=None, n=E_DIRECT) for s, r in dests]
-            continue
-        local = [h for h in range(topo.CHIPS * topo.CORES_PER_CHIP) if topo.chip(h) == topo.chip(c) and h != c]
+        dests = sorted((row.index(j), r) for r, row in enumerate(T.tables["MASK"]) if r != j and j in row)
         taken = []
-        for p in range(PIECES):
-            for s, r in dests:
-                ok = [h for h in local if topo.may_write(h, cores[r])]
-                if VIA[p] == "rank":
-                    pick, n = [h for h in ok if h in cores][0], E_RANK
-                else:
-                    dies = [topo.die(q) for q in taken]
-                    free = [h for h in ok if h not in cores and h not in taken]
-                    free.sort(key=lambda h: (topo.die(h) in dies, topo.die(h) != topo.die(c), h))
-                    pick, n = free[0], E_HELPER
-                    taken.append(pick)
-                flows.append(dict(j=j, r=r, slot=s, lo=p * W, hi=p * W + W, via=pick, n=n))
+        for s, r in dests:
+            via = None
+            if not topo.may_write(c, cores[r]):
+                dies = [topo.die(q) for q in taken]
+                free = [h for h in range(topo.CHIPS * topo.CORES_PER_CHIP)
+                        if topo.chip(h) == topo.chip(c) and topo.may_write(h, cores[r]) and h not in cores and h not in taken]
+                free.sort(key=lambda h: (topo.die(h) in dies, topo.die(h) != topo.die(c), h))
+                via = free[0]
+                taken.append(via)
+            flows.append((j, r, s, via))
     return flows
 
 
@@ -69,55 +61,66 @@ def rank_program(g, core, T, topo):
     cores = list(T.cores)
     S = T.sem
     rank = T.rank_of(core)
-    relay = [f for f in flows if f["via"] == core]
-    if rank is None and not relay:
-        return
-    sent = 0
+    blocks = [(p, p * W, p * W + W) for p in range(NP)]
 
-    if rank is not None:
-        row = T.tables["MASK"][rank]
-        own = row.index(rank)
-        xs = T["xin%d" % own]
-        if PIECES == 1:
-            g.sync.dma_start(T.xd[:], T.x[:]).then_inc(S.staged, 16)
-        g.sync.dma_start(xs[:], T.x[:]).then_inc(S.xl, 16)
-        g.sync.dma_start(T.ws[:], T.w[:]).then_inc(S.wl, 16)
-
-        if PIECES == 1:
-            g.wait_ge(S.staged, 16)
-        else:
-            g.wait_ge(S.xl, 16)
-        mine = [f for f in flows if f["j"] == rank]
-        items, seen = [], []
-        for f in mine:
-            src = T.xd[:] if PIECES == 1 else xs[:, f["lo"]:f["hi"]]
-            if f["via"] is None:
-                items.append((cores[f["r"]], T["xin%d" % f["slot"]][:], src, S["a%d" % f["slot"]], f["n"]))
-            elif (f["via"], f["lo"]) not in seen:
-                seen.append((f["via"], f["lo"]))
-                items.append((f["via"], T.hd[:], src, S.ha, E_HOP1))
-        sent += _send(g, core, T, topo, items)
-
-    if relay:
-        g.wait_ge(S.ha, E_HOP1)
-        sent += _send(g, core, T, topo, [(cores[f["r"]], T["xin%d" % f["slot"]][:, f["lo"]:f["hi"]], T.hd[:],
-                                          S["a%d" % f["slot"]], f["n"]) for f in relay])
-    g.wait_ge(S.sent, sent)
     if rank is None:
+        sent = 0
+        for j, r, s, via in flows:
+            if via == core:
+                for p, lo, hi in blocks:
+                    g.wait_ge(S["ha%d" % p], E_HOP1)
+                    sent += _send(g, core, T, topo, [(cores[r], T["xin%d" % s][:, lo:hi], T.hs[:, lo:hi], S["a%dp%d" % (s, p)], E_HELPER)])
+        if sent:
+            g.wait_ge(S.sent, sent)
         return
 
-    inc = [f for f in flows if f["r"] == rank]
-    late = {s: max(f["via"] is not None for f in inc if f["slot"] == s) for s in range(len(row)) if s != own}
-    order = [own] + sorted(late, key=lambda s: (late[s], s))
-    g.tensor.wait_ge(S.xl, 16)
+    row = T.tables["MASK"][rank]
+    own = row.index(rank)
+    xs = T["xin%d" % own]
+    for p, lo, hi in blocks:
+        g.sync.dma_start(xs[:, lo:hi], T.x[:, lo:hi]).then_inc(S["xl%d" % p], 16)
+    g.sync.dma_start(T.ws[:], T.w[:]).then_inc(S.wl, 16)
+
+    mine = [f for f in flows if f[0] == rank]
+    sent = 0
+    if all(via is None for _, _, _, via in mine):
+        for p, lo, hi in blocks:
+            g.wait_ge(S["xl%d" % p], 16)
+        sent += _send(g, core, T, topo, [(cores[r], T["xin%d" % s][:], xs[:], S["a%dp0" % s], E_DIRECT) for _, r, s, _ in mine])
+    else:
+        for p, lo, hi in blocks:
+            g.wait_ge(S["xl%d" % p], 16)
+            sent += _send(g, core, T, topo, [(via, T.hs[:, lo:hi], xs[:, lo:hi], S["ha%d" % p], E_HOP1) for _, _, _, via in mine])
+    g.wait_ge(S.sent, sent)
+
+    inc = [f for f in flows if f[1] == rank]
+    early = [s for _, _, s, via in inc if via is None]
+    late = [s for _, _, s, via in inc if via is not None]
+    last = (late or early)[-1]
+
+    def product(s, p, lo, hi):
+        mm = g.tensor.matmul(T["ps%d" % p][:, 0:W], T.ws[:, 128 * s:128 * s + 128], T["xin%d" % s][:, lo:hi], s == own, s == last)
+        if s == last:
+            mm.then_inc(S["mm%d" % p], 1)
+
     g.tensor.wait_ge(S.wl, 16)
-    for k, s in enumerate(order):
-        if s != own:
-            g.tensor.wait_ge(S["a%d" % s], sum(f["n"] for f in inc if f["slot"] == s))
-        mm = g.tensor.matmul(T.ps[:], T.ws[:, 128 * s:128 * s + 128], T["xin%d" % s][:], k == 0, k == len(order) - 1)
-    mm.then_inc(S.mm, 1)
-    g.vector.wait_ge(S.mm, 1)
-    g.vector.tensor_copy(T.ys[:], T.ps[:]).then_inc(S.cp, 1)
-    g.sync.wait_ge(S.cp, 1)
-    g.sync.dma_start(T.y[:], T.ys[:]).then_inc(S.st, 16)
-    g.sync.wait_ge(S.st, 16)
+    for p, lo, hi in blocks:
+        g.tensor.wait_ge(S["xl%d" % p], 16)
+        product(own, p, lo, hi)
+    for s in early:
+        g.tensor.wait_ge(S["a%dp0" % s], E_DIRECT)
+        for p, lo, hi in blocks:
+            product(s, p, lo, hi)
+    for p, lo, hi in blocks:
+        for s in late:
+            g.tensor.wait_ge(S["a%dp%d" % (s, p)], E_HELPER)
+            product(s, p, lo, hi)
+
+    for p, lo, hi in blocks:
+        q = g.scalar if p % 2 else g.sync
+        g.vector.wait_ge(S["mm%d" % p], 1)
+        g.vector.tensor_copy(T.ys[:, lo:hi], T["ps%d" % p][:, 0:W]).then_inc(S["cp%d" % p], 1)
+        q.wait_ge(S["cp%d" % p], 1)
+        q.dma_start(T.y[:, lo:hi], T.ys[:, lo:hi]).then_inc(S["st%d" % p], 16)
+    for p, lo, hi in blocks:
+        (g.scalar if p % 2 else g.sync).wait_ge(S["st%d" % p], 16)

@@ -1,11 +1,11 @@
 from concourse.bass import DstId, RemoteDMATransfer
 
 TK = 512
-NP = 2
-W = TK // NP
-E_DIRECT = 4
-E_HOP1 = 8
-E_HELPER = 8
+BLK = {"A": (0, 16), "B": (16, 320), "C": (320, TK)}
+CA = 64
+E_HAND = {"A": 1, "B": 4, "C": 4}
+E_HALF = 4
+E_OUT = 8
 
 SCRATCH = {
     "xin0": ("sbuf", [128, TK], "bfloat16"),
@@ -13,17 +13,24 @@ SCRATCH = {
     "xin2": ("sbuf", [128, TK], "bfloat16"),
     "ws": ("sbuf", [128, 384], "bfloat16"),
     "ys": ("sbuf", [128, TK], "bfloat16"),
-    "hs": ("sbuf", [128, TK], "bfloat16"),
 }
-SEMAPHORES = ["wl", "sent"]
-for _p in range(NP):
+SEMAPHORES = ["wl", "xo", "sent", "st0", "st1"]
+for _b, (_lo, _hi) in BLK.items():
+    SCRATCH["xd" + _b] = ("dram", [128, _hi - _lo], "bfloat16")
+    SCRATCH["hd" + _b] = ("dram", [128, _hi - _lo], "bfloat16")
+    SEMAPHORES += [n + _b for n in ("xl", "ha")]
+SCRATCH["xdS"] = ("dram", [128, CA], "bfloat16")
+SEMAPHORES += ["xlS"]
+for _s in range(3):
+    SCRATCH["rdA%d" % _s] = ("dram", [128, CA], "bfloat16")
+    SEMAPHORES += [n % _s for n in ("aA%d", "aB%d", "aC%d", "cA%d")]
+for _p in range(4):
     SCRATCH["ps%d" % _p] = ("psum", [128, 512], "float32")
-    SEMAPHORES += [n % _p for n in ("xl%d", "ha%d", "a0p%d", "a1p%d", "a2p%d", "mm%d", "cp%d", "st%d")]
+    SEMAPHORES += [n % _p for n in ("mm%d", "cp%d")]
 
 
-def _engines(mask, first, n):
-    bits = [b for b in range(mask.bit_length()) if (mask >> b) & 1]
-    return sum(1 << b for b in bits[first:first + n])
+def _bits(mask):
+    return [b for b in range(mask.bit_length()) if (mask >> b) & 1]
 
 
 def _plan(T, topo):
@@ -45,15 +52,15 @@ def _plan(T, topo):
     return flows
 
 
-def _send(g, core, T, topo, items):
-    trs, first = [], 0
-    for dst, out, src, sem, n in items:
+def _send(g, T, topo, items):
+    trs, n = [], 0
+    for dst, out, src, sem, eng in items:
         rid, pid, _ = topo.addr(dst)
-        trs.append(RemoteDMATransfer(dst_ids=[DstId(rid=rid, pnc=pid)], dma_engine_mask=_engines(topo.mask(core, dst), first, n),
+        trs.append(RemoteDMATransfer(dst_ids=[DstId(rid=rid, pnc=pid)], dma_engine_mask=sum(1 << b for b in eng),
                                      remote_sem=sem, src=src, dst=out))
-        first += n
+        n += len(eng)
     g.remote_dma_fused(trs, local_sem=T.sem.sent)
-    return first
+    return n
 
 
 def rank_program(g, core, T, topo):
@@ -61,15 +68,15 @@ def rank_program(g, core, T, topo):
     cores = list(T.cores)
     S = T.sem
     rank = T.rank_of(core)
-    blocks = [(p, p * W, p * W + W) for p in range(NP)]
 
     if rank is None:
         sent = 0
         for j, r, s, via in flows:
             if via == core:
-                for p, lo, hi in blocks:
-                    g.wait_ge(S["ha%d" % p], E_HOP1)
-                    sent += _send(g, core, T, topo, [(cores[r], T["xin%d" % s][:, lo:hi], T.hs[:, lo:hi], S["a%dp%d" % (s, p)], E_HELPER)])
+                eng = _bits(topo.mask(core, cores[r]))[:E_OUT]
+                for b, (lo, hi) in BLK.items():
+                    g.wait_ge(S["ha" + b], E_HAND[b])
+                    sent += _send(g, T, topo, [(cores[r], T["xin%d" % s][:, lo:hi], T["hd" + b][:], S["a%s%d" % (b, s)], eng)])
         if sent:
             g.wait_ge(S.sent, sent)
         return
@@ -77,50 +84,94 @@ def rank_program(g, core, T, topo):
     row = T.tables["MASK"][rank]
     own = row.index(rank)
     xs = T["xin%d" % own]
-    for p, lo, hi in blocks:
-        g.sync.dma_start(xs[:, lo:hi], T.x[:, lo:hi]).then_inc(S["xl%d" % p], 16)
+    mine = [f for f in flows if f[0] == rank]
+    inc = [f for f in flows if f[1] == rank]
+    relayed = any(via is not None for _, _, _, via in mine)
+
+    if relayed:
+        for b in BLK:
+            g.sync.dma_start(T["xd" + b][:], T.x[:, BLK[b][0]:BLK[b][1]]).then_inc(S["xl" + b], 16)
+        g.sync.dma_start(xs[:], T.x[:]).then_inc(S.xo, 16)
+    else:
+        g.sync.dma_start(T.xdS[:], T.x[:, 0:CA]).then_inc(S.xlS, 16)
+        g.sync.dma_start(xs[:, CA:TK], T.x[:, CA:TK]).then_inc(S.xlB, 16)
+        g.sync.dma_start(xs[:, 0:CA], T.x[:, 0:CA]).then_inc(S.xo, 16)
     g.sync.dma_start(T.ws[:], T.w[:]).then_inc(S.wl, 16)
 
-    mine = [f for f in flows if f[0] == rank]
     sent = 0
-    if all(via is None for _, _, _, via in mine):
-        for p, lo, hi in blocks:
-            g.wait_ge(S["xl%d" % p], 16)
-        sent += _send(g, core, T, topo, [(cores[r], T["xin%d" % s][:], xs[:], S["a%dp0" % s], E_DIRECT) for _, r, s, _ in mine])
+    if relayed:
+        for b in BLK:
+            g.wait_ge(S["xl" + b], 16)
+            items = []
+            for k, (_, _, _, via) in enumerate(mine):
+                eng = _bits(topo.mask(core, via))[0::2]
+                share = len(eng) // len(mine)
+                items.append((via, T["hd" + b][:], T["xd" + b][:], S["ha" + b], eng[k * share:k * share + E_HAND[b]]))
+            sent += _send(g, T, topo, items)
     else:
-        for p, lo, hi in blocks:
-            g.wait_ge(S["xl%d" % p], 16)
-            sent += _send(g, core, T, topo, [(via, T.hs[:, lo:hi], xs[:, lo:hi], S["ha%d" % p], E_HOP1) for _, _, _, via in mine])
+        for first in (True, False):
+            g.wait_ge(S.xlS if first else S.xlB, 16)
+            items = []
+            for k, (_, r, s, _) in enumerate(mine):
+                eng = _bits(topo.mask(core, cores[r]))[k * E_HALF:(k + 1) * E_HALF]
+                if first:
+                    items.append((cores[r], T["rdA%d" % s][:], T.xdS[:], S["aA%d" % s], eng))
+                else:
+                    items.append((cores[r], T["xin%d" % s][:, CA:TK], xs[:, CA:TK], S["aB%d" % s], eng))
+            sent += _send(g, T, topo, items)
     g.wait_ge(S.sent, sent)
 
-    inc = [f for f in flows if f[1] == rank]
     early = [s for _, _, s, via in inc if via is None]
     late = [s for _, _, s, via in inc if via is not None]
-    last = (late or early)[-1]
+    for k, s in enumerate(early):
+        q = g.scalar if k % 2 else g.sync
+        q.wait_ge(S["aA%d" % s], E_HALF)
+        q.dma_start(T["xin%d" % s][:, 0:CA], T["rdA%d" % s][:]).then_inc(S["cA%d" % s], 16)
 
-    def product(s, p, lo, hi):
-        mm = g.tensor.matmul(T["ps%d" % p][:, 0:W], T.ws[:, 128 * s:128 * s + 128], T["xin%d" % s][:, lo:hi], s == own, s == last)
-        if s == last:
+    pieces = {own: [(0, TK, S.wl, 16), (0, TK, S.xo, 16)] + ([] if relayed else [(CA, TK, S.xlB, 16)])}
+    for s in early:
+        pieces[s] = [(0, CA, S["cA%d" % s], 16), (CA, TK, S["aB%d" % s], E_HALF)]
+    for s in late:
+        pieces[s] = [(lo, hi, S["a%s%d" % (b, s)], E_OUT) for b, (lo, hi) in BLK.items()]
+
+    if late:
+        mid = (BLK["C"][0] + TK) // 2
+        banks = [BLK["A"], BLK["B"], (BLK["C"][0], mid), (mid, TK)]
+        stores = [[0, 1], [2, 3]]
+    else:
+        banks = [(0, TK // 2), (TK // 2, 3 * TK // 4), (3 * TK // 4, TK)]
+        stores = [[0], [1, 2]]
+    nb = range(len(banks))
+    ops = [(own, p) for p in nb]
+    if late:
+        ops += [(s, p) for s in early for p in nb]
+    else:
+        ops += [(s, p) for p in nb for s in early]
+    ops += [(s, p) for p in nb for s in late]
+    last = {}
+    for i, (s, p) in enumerate(ops):
+        last[p] = i
+    waited = []
+    for i, (s, p) in enumerate(ops):
+        lo, hi = banks[p]
+        for k, (a, z, sem, n) in enumerate(pieces[s]):
+            if a < hi and lo < z and (s, k) not in waited:
+                g.tensor.wait_ge(sem, n)
+                waited.append((s, k))
+        mm = g.tensor.matmul(T["ps%d" % p][:, 0:hi - lo], T.ws[:, 128 * s:128 * s + 128], T["xin%d" % s][:, lo:hi], s == own, last[p] == i)
+        if last[p] == i:
             mm.then_inc(S["mm%d" % p], 1)
 
-    g.tensor.wait_ge(S.wl, 16)
-    for p, lo, hi in blocks:
-        g.tensor.wait_ge(S["xl%d" % p], 16)
-        product(own, p, lo, hi)
-    for s in early:
-        g.tensor.wait_ge(S["a%dp0" % s], E_DIRECT)
-        for p, lo, hi in blocks:
-            product(s, p, lo, hi)
-    for p, lo, hi in blocks:
-        for s in late:
-            g.tensor.wait_ge(S["a%dp%d" % (s, p)], E_HELPER)
-            product(s, p, lo, hi)
-
-    for p, lo, hi in blocks:
-        q = g.scalar if p % 2 else g.sync
+    for p in nb:
+        lo, hi = banks[p]
         g.vector.wait_ge(S["mm%d" % p], 1)
-        g.vector.tensor_copy(T.ys[:, lo:hi], T["ps%d" % p][:, 0:W]).then_inc(S["cp%d" % p], 1)
-        q.wait_ge(S["cp%d" % p], 1)
-        q.dma_start(T.y[:, lo:hi], T.ys[:, lo:hi]).then_inc(S["st%d" % p], 16)
-    for p, lo, hi in blocks:
-        (g.scalar if p % 2 else g.sync).wait_ge(S["st%d" % p], 16)
+        g.vector.tensor_copy(T.ys[:, lo:hi], T["ps%d" % p][:, 0:hi - lo]).then_inc(S["cp%d" % p], 1)
+
+    for k, group in enumerate(stores):
+        q = g.scalar if k % 2 else g.sync
+        for p in group:
+            q.wait_ge(S["cp%d" % p], 1)
+        lo, hi = banks[group[0]][0], banks[group[-1]][1]
+        q.dma_start(T.y[:, lo:hi], T.ys[:, lo:hi]).then_inc(S["st%d" % k], 16)
+    g.sync.wait_ge(S.st0, 16)
+    g.scalar.wait_ge(S.st1, 16)

from concourse.bass import DstId, RemoteDMATransfer

TK = 512
BLK = {"A": (0, 16), "B": (16, 320), "C": (320, TK)}
CA = 64
E_HAND = {"A": 1, "B": 4, "C": 4}
E_HALF = 4
E_OUT = 8

SCRATCH = {
    "xin0": ("sbuf", [128, TK], "bfloat16"),
    "xin1": ("sbuf", [128, TK], "bfloat16"),
    "xin2": ("sbuf", [128, TK], "bfloat16"),
    "ws": ("sbuf", [128, 384], "bfloat16"),
    "ys": ("sbuf", [128, TK], "bfloat16"),
}
SEMAPHORES = ["wl", "xo", "sent", "st0", "st1"]
for _b, (_lo, _hi) in BLK.items():
    SCRATCH["xd" + _b] = ("dram", [128, _hi - _lo], "bfloat16")
    SCRATCH["hd" + _b] = ("dram", [128, _hi - _lo], "bfloat16")
    SEMAPHORES += [n + _b for n in ("xl", "ha")]
SCRATCH["xdS"] = ("dram", [128, CA], "bfloat16")
SEMAPHORES += ["xlS"]
for _s in range(3):
    SCRATCH["rdA%d" % _s] = ("dram", [128, CA], "bfloat16")
    SEMAPHORES += [n % _s for n in ("aA%d", "aB%d", "aC%d", "cA%d")]
for _p in range(4):
    SCRATCH["ps%d" % _p] = ("psum", [128, 512], "float32")
    SEMAPHORES += [n % _p for n in ("mm%d", "cp%d")]


def _bits(mask):
    return [b for b in range(mask.bit_length()) if (mask >> b) & 1]


def _plan(T, topo):
    cores = list(T.cores)
    flows = []
    for j, c in enumerate(cores):
        dests = sorted((row.index(j), r) for r, row in enumerate(T.tables["MASK"]) if r != j and j in row)
        taken = []
        for s, r in dests:
            via = None
            if not topo.may_write(c, cores[r]):
                dies = [topo.die(q) for q in taken]
                free = [h for h in range(topo.CHIPS * topo.CORES_PER_CHIP)
                        if topo.chip(h) == topo.chip(c) and topo.may_write(h, cores[r]) and h not in cores and h not in taken]
                free.sort(key=lambda h: (topo.die(h) in dies, topo.die(h) != topo.die(c), h))
                via = free[0]
                taken.append(via)
            flows.append((j, r, s, via))
    return flows


def _send(g, T, topo, items):
    trs, n = [], 0
    for dst, out, src, sem, eng in items:
        rid, pid, _ = topo.addr(dst)
        trs.append(RemoteDMATransfer(dst_ids=[DstId(rid=rid, pnc=pid)], dma_engine_mask=sum(1 << b for b in eng),
                                     remote_sem=sem, src=src, dst=out))
        n += len(eng)
    g.remote_dma_fused(trs, local_sem=T.sem.sent)
    return n


def rank_program(g, core, T, topo):
    flows = _plan(T, topo)
    cores = list(T.cores)
    S = T.sem
    rank = T.rank_of(core)

    if rank is None:
        sent = 0
        for j, r, s, via in flows:
            if via == core:
                eng = _bits(topo.mask(core, cores[r]))[:E_OUT]
                for b, (lo, hi) in BLK.items():
                    g.wait_ge(S["ha" + b], E_HAND[b])
                    sent += _send(g, T, topo, [(cores[r], T["xin%d" % s][:, lo:hi], T["hd" + b][:], S["a%s%d" % (b, s)], eng)])
        if sent:
            g.wait_ge(S.sent, sent)
        return

    row = T.tables["MASK"][rank]
    own = row.index(rank)
    xs = T["xin%d" % own]
    mine = [f for f in flows if f[0] == rank]
    inc = [f for f in flows if f[1] == rank]
    relayed = any(via is not None for _, _, _, via in mine)

    if relayed:
        for b in BLK:
            g.sync.dma_start(T["xd" + b][:], T.x[:, BLK[b][0]:BLK[b][1]]).then_inc(S["xl" + b], 16)
        g.sync.dma_start(xs[:], T.x[:]).then_inc(S.xo, 16)
    else:
        g.sync.dma_start(T.xdS[:], T.x[:, 0:CA]).then_inc(S.xlS, 16)
        g.sync.dma_start(xs[:, CA:TK], T.x[:, CA:TK]).then_inc(S.xlB, 16)
        g.sync.dma_start(xs[:, 0:CA], T.x[:, 0:CA]).then_inc(S.xo, 16)
    g.sync.dma_start(T.ws[:], T.w[:]).then_inc(S.wl, 16)

    sent = 0
    if relayed:
        for b in BLK:
            g.wait_ge(S["xl" + b], 16)
            items = []
            for k, (_, _, _, via) in enumerate(mine):
                eng = _bits(topo.mask(core, via))[0::2]
                share = len(eng) // len(mine)
                items.append((via, T["hd" + b][:], T["xd" + b][:], S["ha" + b], eng[k * share:k * share + E_HAND[b]]))
            sent += _send(g, T, topo, items)
    else:
        for first in (True, False):
            g.wait_ge(S.xlS if first else S.xlB, 16)
            items = []
            for k, (_, r, s, _) in enumerate(mine):
                eng = _bits(topo.mask(core, cores[r]))[k * E_HALF:(k + 1) * E_HALF]
                if first:
                    items.append((cores[r], T["rdA%d" % s][:], T.xdS[:], S["aA%d" % s], eng))
                else:
                    items.append((cores[r], T["xin%d" % s][:, CA:TK], xs[:, CA:TK], S["aB%d" % s], eng))
            sent += _send(g, T, topo, items)
    g.wait_ge(S.sent, sent)

    early = [s for _, _, s, via in inc if via is None]
    late = [s for _, _, s, via in inc if via is not None]
    for k, s in enumerate(early):
        q = g.scalar if k % 2 else g.sync
        q.wait_ge(S["aA%d" % s], E_HALF)
        q.dma_start(T["xin%d" % s][:, 0:CA], T["rdA%d" % s][:]).then_inc(S["cA%d" % s], 16)

    pieces = {own: [(0, TK, S.wl, 16), (0, TK, S.xo, 16)] + ([] if relayed else [(CA, TK, S.xlB, 16)])}
    for s in early:
        pieces[s] = [(0, CA, S["cA%d" % s], 16), (CA, TK, S["aB%d" % s], E_HALF)]
    for s in late:
        pieces[s] = [(lo, hi, S["a%s%d" % (b, s)], E_OUT) for b, (lo, hi) in BLK.items()]

    if late:
        mid = (BLK["C"][0] + TK) // 2
        banks = [BLK["A"], BLK["B"], (BLK["C"][0], mid), (mid, TK)]
        stores = [[0, 1], [2, 3]]
    else:
        banks = [(0, TK // 2), (TK // 2, 3 * TK // 4), (3 * TK // 4, TK)]
        stores = [[0], [1, 2]]
    nb = range(len(banks))
    ops = [(own, p) for p in nb]
    if late:
        ops += [(s, p) for s in early for p in nb]
    else:
        ops += [(s, p) for p in nb for s in early]
    ops += [(s, p) for p in nb for s in late]
    last = {}
    for i, (s, p) in enumerate(ops):
        last[p] = i
    waited = []
    for i, (s, p) in enumerate(ops):
        lo, hi = banks[p]
        for k, (a, z, sem, n) in enumerate(pieces[s]):
            if a < hi and lo < z and (s, k) not in waited:
                g.tensor.wait_ge(sem, n)
                waited.append((s, k))
        mm = g.tensor.matmul(T["ps%d" % p][:, 0:hi - lo], T.ws[:, 128 * s:128 * s + 128], T["xin%d" % s][:, lo:hi], s == own, last[p] == i)
        if last[p] == i:
            mm.then_inc(S["mm%d" % p], 1)

    for p in nb:
        lo, hi = banks[p]
        g.vector.wait_ge(S["mm%d" % p], 1)
        g.vector.tensor_copy(T.ys[:, lo:hi], T["ps%d" % p][:, 0:hi - lo]).then_inc(S["cp%d" % p], 1)

    for k, group in enumerate(stores):
        q = g.scalar if k % 2 else g.sync
        for p in group:
            q.wait_ge(S["cp%d" % p], 1)
        lo, hi = banks[group[0]][0], banks[group[-1]][1]
        q.dma_start(T.y[:, lo:hi], T.ys[:, lo:hi]).then_inc(S["st%d" % k], 16)
    g.sync.wait_ge(S.st0, 16)
    g.scalar.wait_ge(S.st1, 16)
